import numpy as np, ml_dtypes
CORES = [16,32,48,64,80]
N = 5
import mx_ref
NC = 256
BF = ml_dtypes.bfloat16
def setup_inputs(rng):
    def f(*shape):
        return mx_ref.flush((rng.standard_normal(shape, dtype=np.float32) * np.exp2(rng.integers(-2, 3, shape[:-1] + (1,)))).astype(BF))
    return {"w": f(N, 128, N * 512), "x": f(N, 128, N * 4 * NC)}
def setup_inputs_blocks(rng):
    d = setup_inputs(rng)
    for k in ("w", "x"): d[k] = mx_ref.spread(d[k], rng, 2)
    return d
def setup_inputs_wide(rng):
    d = setup_inputs(rng)
    for k in ("w", "x"): d[k] = mx_ref.flush((d[k].astype(np.float32) * np.exp2(rng.integers(-8, 9, (N, 1, 1))).astype(np.float32)).astype(BF))
    return d
def setup_inputs_zeros(rng):
    d = setup_inputs(rng); v = d["x"].reshape(N, 128, -1, 4).copy()
    v[np.broadcast_to((rng.random((N, 1, v.shape[2], 1)) < 0.33), v.shape)] = 0
    d["x"] = v.reshape(d["x"].shape)
    return d
def reference(w, x):
    y = np.zeros((N, 128, NC), np.float32)
    for r in range(N):
        for j in range(N):
            p = mx_ref.matmul(mx_ref.quantize(w[r][:, 512 * j:512 * j + 512]), mx_ref.quantize(x[j][:, 4 * NC * r:4 * NC * r + 4 * NC]))
            y[r] = p if j == 0 else y[r] + p
    return {"y": y}

@@ -1,0 +1,128 @@
+from concourse.mybir import dt
+
+N = 5
+SIM_CORES = 96
+XE, XC = 1024, 256
+WE, WC = 512, 128
+FORWARD = 0
+
+SCRATCH = {
+    "xb": ("sbuf", [128, N * XE], "bfloat16"),
+    "wb": ("sbuf", [128, N * WE], "bfloat16"),
+    "xq": ("sbuf", [128, N * XC], "float8_e4m3fn_x4"),
+    "xs": ("sbuf", [128, N * XC], "uint8"),
+    "wq": ("sbuf", [128, N * WC], "float8_e4m3fn_x4"),
+    "ws": ("sbuf", [128, N * WC], "uint8"),
+    "rq": ("sbuf", [128, N * XC], "float8_e4m3fn_x4"),
+    "rs": ("sbuf", [128, N * XC], "uint8"),
+    "acc": ("psum", [128, 512], "float32"),
+    "yo": ("sbuf", [128, XC], "float32"),
+}
+SEMAPHORES = (["lx%d" % i for i in range(N)] + ["qx%d" % i for i in range(N)] + ["qw%d" % i for i in range(N)]
+              + ["arr%d" % i for i in range(N)] + ["lw", "sent", "mm", "cp", "st", "hq", "hs"])
+
+
+def _engines(mask):
+    return bin(mask).count("1")
+
+
+def _forwarders(home, topo):
+    return [c for c in range(SIM_CORES) if topo.chip(c) == topo.chip(home) and topo.die(c) != topo.die(home)]
+
+
+def _send(g, T, topo, src, dst, mask, out_q, in_q, out_s, in_s, sem_q, sem_s):
+    rid, pid, _ = topo.addr(dst)
+    g.remote_dma(out_ap=out_s, in_ap=in_s, remote_sem=sem_s, local_sem=T.sem.sent, pid=pid, routing_id=rid,
+                 dma_engine_mask=mask)
+    g.remote_dma(out_ap=out_q.bitcast(dt.uint8), in_ap=in_q.bitcast(dt.uint8), remote_sem=sem_q,
+                 local_sem=T.sem.sent, pid=pid, routing_id=rid, dma_engine_mask=mask)
+    return 2 * _engines(mask)
+
+
+def _forward_program(g, core, T, topo):
+    homes = [c for c in T.cores if topo.chip(c) == topo.chip(core)]
+    if not homes:
+        return
+    home = homes[0]
+    mine = _forwarders(home, topo)[:FORWARD]
+    if core not in mine:
+        return
+    j = T.rank_of(home)
+    dst = T.cores[(j + 1 + mine.index(core)) % N]
+    came = _engines(topo.mask(home, core) & ~topo.mask(home, dst))
+    mask = topo.mask(core, dst)
+    rid, pid, _ = topo.addr(dst)
+    slot = slice(XC * j, XC * (j + 1))
+    arr = T.sem["arr%d" % j]
+    g.wait_ge(T.sem.hs, came)
+    g.remote_dma(out_ap=T.rs[:, slot], in_ap=T.rs[:, slot], remote_sem=arr, local_sem=T.sem.sent, pid=pid,
+                 routing_id=rid, dma_engine_mask=mask)
+    g.wait_ge(T.sem.hq, came)
+    g.remote_dma(out_ap=T.rq[:, slot].bitcast(dt.uint8), in_ap=T.rq[:, slot].bitcast(dt.uint8), remote_sem=arr,
+                 local_sem=T.sem.sent, pid=pid, routing_id=rid, dma_engine_mask=mask)
+    g.wait_ge(T.sem.sent, 2 * _engines(mask))
+
+
+def rank_program(g, core, T, topo):
+    rank = T.rank_of(core)
+    if rank is None:
+        _forward_program(g, core, T, topo)
+        return
+    sem = T.sem
+    order = [(rank + k) % N for k in range(1, N)] + [rank]
+
+    queues = [g.sync, g.scalar]
+    for i, r in enumerate(order):
+        cols = slice(XE * r, XE * (r + 1))
+        queues[i % 2].dma_start(T.xb[:, cols], T.x[:, cols]).then_inc(sem["lx%d" % r], 16)
+    queues[N % 2].dma_start(T.wb[:], T.w[:]).then_inc(sem.lw, 16)
+
+    rounds = list(range(FORWARD + 1, N))
+    rounds = rounds[:-1] + list(range(1, FORWARD + 1)) + rounds[-1:]
+    seq = [rank] + [(rank - k) % N for k in rounds]
+
+    for r in order:
+        g.vector.wait_ge(sem["lx%d" % r], 16)
+        g.vector.quantize_mx(T.xq[:, XC * r:XC * (r + 1)], T.xs[:, XC * r:XC * (r + 1)],
+                             T.xb[:, XE * r:XE * (r + 1)]).then_inc(sem["qx%d" % r], 1)
+    g.vector.wait_ge(sem.lw, 16)
+    for j in seq:
+        g.vector.quantize_mx(T.wq[:, WC * j:WC * (j + 1)], T.ws[:, WC * j:WC * (j + 1)],
+                             T.wb[:, WE * j:WE * (j + 1)]).then_inc(sem["qw%d" % j], 1)
+
+    helpers = _forwarders(core, topo)
+    land = slice(XC * rank, XC * (rank + 1))
+    left = 0
+    for k, r in enumerate(order[:-1]):
+        dst = T.cores[r]
+        mine = slice(XC * r, XC * (r + 1))
+        g.wait_ge(sem["qx%d" % r], 1)
+        if k < FORWARD:
+            via = helpers[k]
+            spare = topo.mask(core, via) & ~topo.mask(core, dst)
+            left += _send(g, T, topo, core, via, spare, T.rq[:, land], T.xq[:, mine], T.rs[:, land],
+                          T.xs[:, mine], sem.hq, sem.hs)
+        else:
+            arr = sem["arr%d" % rank]
+            left += _send(g, T, topo, core, dst, topo.mask(core, dst), T.rq[:, land], T.xq[:, mine],
+                          T.rs[:, land], T.xs[:, mine], arr, arr)
+
+    for i, j in enumerate(seq):
+        g.tensor.wait_ge(sem["qw%d" % j], 1)
+        slot = slice(XC * j, XC * (j + 1))
+        if j == rank:
+            g.tensor.wait_ge(sem["qx%d" % j], 1)
+            codes, plane = T.xq[:, slot], T.xs[:, slot]
+        else:
+            g.tensor.wait_ge(sem["arr%d" % j], 2 * _engines(topo.mask(T.cores[j], core)))
+            codes, plane = T.rq[:, slot], T.rs[:, slot]
+        mm = g.tensor.matmul_mx(T.acc[:, 0:XC], T.wq[:, WC * j:WC * (j + 1)], T.ws[:, WC * j:WC * (j + 1)],
+                                codes, plane, i == 0, i == N - 1)
+    mm.then_inc(sem.mm, 1)
+
+    g.vector.wait_ge(sem.mm, 1)
+    g.vector.tensor_copy(T.yo[:], T.acc[:, 0:XC]).then_inc(sem.cp, 1)
+    g.sync.wait_ge(sem.cp, 1)
+    g.sync.dma_start(T.y[:], T.yo[:]).then_inc(sem.st, 16)
+    g.sync.wait_ge(sem.st, 16)
+    g.wait_ge(sem.sent, left)

@@ -4,7 +4,7 @@ N = 5
 SIM_CORES = 96
 XE, XC = 1024, 256
 WE, WC = 512, 128
-FORWARD = 0
+FORWARD = 1
 
 SCRATCH = {
     "xb": ("sbuf", [128, N * XE], "bfloat16"),

from concourse.mybir import dt

N = 5
SIM_CORES = 96
XE, XC = 1024, 256
WE, WC = 512, 128
FORWARD = 1

SCRATCH = {
    "xb": ("sbuf", [128, N * XE], "bfloat16"),
    "wb": ("sbuf", [128, N * WE], "bfloat16"),
    "xq": ("sbuf", [128, N * XC], "float8_e4m3fn_x4"),
    "xs": ("sbuf", [128, N * XC], "uint8"),
    "wq": ("sbuf", [128, N * WC], "float8_e4m3fn_x4"),
    "ws": ("sbuf", [128, N * WC], "uint8"),
    "rq": ("sbuf", [128, N * XC], "float8_e4m3fn_x4"),
    "rs": ("sbuf", [128, N * XC], "uint8"),
    "acc": ("psum", [128, 512], "float32"),
    "yo": ("sbuf", [128, XC], "float32"),
}
SEMAPHORES = (["lx%d" % i for i in range(N)] + ["qx%d" % i for i in range(N)] + ["qw%d" % i for i in range(N)]
              + ["arr%d" % i for i in range(N)] + ["lw", "sent", "mm", "cp", "st", "hq", "hs"])


def _engines(mask):
    return bin(mask).count("1")


def _forwarders(home, topo):
    return [c for c in range(SIM_CORES) if topo.chip(c) == topo.chip(home) and topo.die(c) != topo.die(home)]


def _send(g, T, topo, src, dst, mask, out_q, in_q, out_s, in_s, sem_q, sem_s):
    rid, pid, _ = topo.addr(dst)
    g.remote_dma(out_ap=out_s, in_ap=in_s, remote_sem=sem_s, local_sem=T.sem.sent, pid=pid, routing_id=rid,
                 dma_engine_mask=mask)
    g.remote_dma(out_ap=out_q.bitcast(dt.uint8), in_ap=in_q.bitcast(dt.uint8), remote_sem=sem_q,
                 local_sem=T.sem.sent, pid=pid, routing_id=rid, dma_engine_mask=mask)
    return 2 * _engines(mask)


def _forward_program(g, core, T, topo):
    homes = [c for c in T.cores if topo.chip(c) == topo.chip(core)]
    if not homes:
        return
    home = homes[0]
    mine = _forwarders(home, topo)[:FORWARD]
    if core not in mine:
        return
    j = T.rank_of(home)
    dst = T.cores[(j + 1 + mine.index(core)) % N]
    came = _engines(topo.mask(home, core) & ~topo.mask(home, dst))
    mask = topo.mask(core, dst)
    rid, pid, _ = topo.addr(dst)
    slot = slice(XC * j, XC * (j + 1))
    arr = T.sem["arr%d" % j]
    g.wait_ge(T.sem.hs, came)
    g.remote_dma(out_ap=T.rs[:, slot], in_ap=T.rs[:, slot], remote_sem=arr, local_sem=T.sem.sent, pid=pid,
                 routing_id=rid, dma_engine_mask=mask)
    g.wait_ge(T.sem.hq, came)
    g.remote_dma(out_ap=T.rq[:, slot].bitcast(dt.uint8), in_ap=T.rq[:, slot].bitcast(dt.uint8), remote_sem=arr,
                 local_sem=T.sem.sent, pid=pid, routing_id=rid, dma_engine_mask=mask)
    g.wait_ge(T.sem.sent, 2 * _engines(mask))


def rank_program(g, core, T, topo):
    rank = T.rank_of(core)
    if rank is None:
        _forward_program(g, core, T, topo)
        return
    sem = T.sem
    order = [(rank + k) % N for k in range(1, N)] + [rank]

    queues = [g.sync, g.scalar]
    for i, r in enumerate(order):
        cols = slice(XE * r, XE * (r + 1))
        queues[i % 2].dma_start(T.xb[:, cols], T.x[:, cols]).then_inc(sem["lx%d" % r], 16)
    queues[N % 2].dma_start(T.wb[:], T.w[:]).then_inc(sem.lw, 16)

    rounds = list(range(FORWARD + 1, N))
    rounds = rounds[:-1] + list(range(1, FORWARD + 1)) + rounds[-1:]
    seq = [rank] + [(rank - k) % N for k in rounds]

    for r in order:
        g.vector.wait_ge(sem["lx%d" % r], 16)
        g.vector.quantize_mx(T.xq[:, XC * r:XC * (r + 1)], T.xs[:, XC * r:XC * (r + 1)],
                             T.xb[:, XE * r:XE * (r + 1)]).then_inc(sem["qx%d" % r], 1)
    g.vector.wait_ge(sem.lw, 16)
    for j in seq:
        g.vector.quantize_mx(T.wq[:, WC * j:WC * (j + 1)], T.ws[:, WC * j:WC * (j + 1)],
                             T.wb[:, WE * j:WE * (j + 1)]).then_inc(sem["qw%d" % j], 1)

    helpers = _forwarders(core, topo)
    land = slice(XC * rank, XC * (rank + 1))
    left = 0
    for k, r in enumerate(order[:-1]):
        dst = T.cores[r]
        mine = slice(XC * r, XC * (r + 1))
        g.wait_ge(sem["qx%d" % r], 1)
        if k < FORWARD:
            via = helpers[k]
            spare = topo.mask(core, via) & ~topo.mask(core, dst)
            left += _send(g, T, topo, core, via, spare, T.rq[:, land], T.xq[:, mine], T.rs[:, land],
                          T.xs[:, mine], sem.hq, sem.hs)
        else:
            arr = sem["arr%d" % rank]
            left += _send(g, T, topo, core, dst, topo.mask(core, dst), T.rq[:, land], T.xq[:, mine],
                          T.rs[:, land], T.xs[:, mine], arr, arr)

    for i, j in enumerate(seq):
        g.tensor.wait_ge(sem["qw%d" % j], 1)
        slot = slice(XC * j, XC * (j + 1))
        if j == rank:
            g.tensor.wait_ge(sem["qx%d" % j], 1)
            codes, plane = T.xq[:, slot], T.xs[:, slot]
        else:
            g.tensor.wait_ge(sem["arr%d" % j], 2 * _engines(topo.mask(T.cores[j], core)))
            codes, plane = T.rq[:, slot], T.rs[:, slot]
        mm = g.tensor.matmul_mx(T.acc[:, 0:XC], T.wq[:, WC * j:WC * (j + 1)], T.ws[:, WC * j:WC * (j + 1)],
                                codes, plane, i == 0, i == N - 1)
    mm.then_inc(sem.mm, 1)

    g.vector.wait_ge(sem.mm, 1)
    g.vector.tensor_copy(T.yo[:], T.acc[:, 0:XC]).then_inc(sem.cp, 1)
    g.sync.wait_ge(sem.cp, 1)
    g.sync.dma_start(T.y[:], T.yo[:]).then_inc(sem.st, 16)
    g.sync.wait_ge(sem.st, 16)
    g.wait_ge(sem.sent, left)
